import numpy as np, ml_dtypes
CORES = [40,42,43,45,46]
N = 5
import mx_ref
BF = ml_dtypes.bfloat16
def pick(q, e):
    c = np.concatenate([q[0].reshape(128, -1, 4), np.zeros((128, 1, 4), np.uint8)], axis=1); s = np.concatenate([q[1], np.ones((16, 1), np.uint8)], axis=1)
    return (np.ascontiguousarray(c[:, e].reshape(128, -1)), np.ascontiguousarray(s[:, e]))
def join(*qs):
    return (np.concatenate([q[0] for q in qs], axis=1), np.concatenate([q[1] for q in qs], axis=1))
def put(q, e, v):
    c, s = q[0].reshape(128, -1, 4).copy(), q[1].copy(); c[:, e] = v[0].reshape(128, -1, 4); s[:, e] = v[1]
    return (c.reshape(128, -1), s)
def pk(c, s):
    return (np.ascontiguousarray(c), mx_ref.live(s))
def emit(q):
    return q[0], q[1]
def decode(q):
    o = []
    for b in range(4):
        e = np.zeros((128, 128, 4), np.float32); e[np.arange(128), np.arange(128), b] = 1
        o.append(mx_ref.matmul(mx_ref.quantize(e.reshape(128, 512).astype(BF)), q))
    return np.stack(o, axis=2).reshape(128, -1)
def f(rng, *shape):
    return mx_ref.flush((rng.standard_normal(shape, dtype=np.float32) * np.exp2(rng.integers(-2, 3, shape[:-1] + (1,)))).astype(BF))
def wide(rng, *shape, cols=0):
    v = rng.standard_normal(shape, dtype=np.float32) * np.exp2(rng.integers(-12, 13, shape)).astype(np.float32)
    if cols: v *= np.repeat(np.exp2(rng.integers(-cols, cols + 1, shape[:-2] + (1, shape[-1] // 4))) * (rng.random(shape[:-2] + (1, shape[-1] // 4)) > 0.0625), 4, axis=-1).astype(np.float32)
    return mx_ref.flush(v.astype(BF))
P, K, R = 192, 48, 3
def lift(v):
    v = np.asarray(v).astype(np.float32)
    v[np.abs(v) < np.float32(2.0 ** -16)] = 0
    return v.astype(BF)
def whole(x, hc, u, w):
    i = np.arange(N)
    return {"x": x, "hl": hc[(i - 1) % N], "hc": hc, "hr": hc[(i + 1) % N], "u": u, "w": w}
def query(rng):
    v = np.zeros((N, 128, 512), BF)
    v[:, :, :4] = f(rng, 128, 4)
    return v
def near(rng, hc):
    k = np.repeat(np.exp2(rng.integers(-3, 2, (N, 1, P))), 4, axis=2)
    return lift(hc.astype(np.float32) + f(rng, N, 128, 4 * P).astype(np.float32) * k)
def setup_inputs(rng):
    hc = lift(f(rng, N, 128, 4 * P))
    return whole(near(rng, hc), hc, query(rng), f(rng, N, 128, 512))
def setup_inputs_spread(rng):
    hc = lift(wide(rng, N, 128, 4 * P, cols=4))
    return whole(lift(wide(rng, N, 128, 4 * P, cols=4)), hc, query(rng), f(rng, N, 128, 512))
def setup_inputs_ties(rng):
    d = setup_inputs(rng)
    g = rng.permutation(P) // 7
    s = np.repeat(1 - 2 * rng.integers(0, 2, P), 4).astype(np.float32)
    def same(v):
        return (v.reshape(N, 128, P, 4)[:, :, g].reshape(N, 128, 4 * P).astype(np.float32) * s).astype(BF)
    return whole(same(d["x"]), same(d["hc"]), d["u"], d["w"])
def setup_inputs_again(rng):
    d = setup_inputs(rng)
    k = np.ones(P, np.float32)
    k[rng.permutation(P)[:K]] = 1024
    k = np.repeat(k, 4)
    return whole(lift(d["x"].astype(np.float32) * k), lift(d["hc"].astype(np.float32) * k), d["u"], d["w"])
def setup_inputs_still(rng):
    d = setup_inputs(rng)
    v = rng.integers(128, 256, (16, 8, P, 4)) * np.exp2(rng.integers(-10, -7, (16, 8, P, 4)))
    v[:, 0, :, 0] = (128 + 8 * np.argsort(rng.random((16, P)), axis=0) + rng.integers(1, 8, (16, P))) * 2.0 ** -7
    v = v * rng.choice([-1.0, 1.0], v.shape) * np.exp2(rng.integers(-2, 3, (16, 1, P, 1)))
    v = v.reshape(128, 4 * P).astype(np.float32).astype(BF)
    held = decode(mx_ref.quantize(v)).astype(BF)
    s = int(rng.integers(0, N))
    hc = np.array(d["hc"])
    for r in range(s - 1, s + 3): hc[r % N] = v
    x = near(rng, hc)
    x[s] = held
    few = np.array(x[(s + 1) % N]).reshape(128, P, 4)
    rest = rng.permutation(P)[K // 2:]
    few[:, rest] = held.reshape(128, P, 4)[:, rest]
    x[(s + 1) % N] = few.reshape(128, 4 * P)
    return whole(x, hc, d["u"], d["w"])
def setup_inputs_one(rng):
    d = setup_inputs(rng)
    p, t = int(rng.integers(0, 128)), int(rng.integers(0, 4))
    u = np.zeros((N, 128, 512), BF)
    u[:, p, t] = -1.5
    off = np.sort(rng.permutation(P)[K // 2:])
    x, hc = np.array(d["x"]).reshape(N, 128, P, 4), np.array(d["hc"]).reshape(N, 128, P, 4)
    x[:, :, off[::2]] = (x[:, :, off[::2]].astype(np.float32) - np.float32(128)).astype(BF)
    x[:, p, off, t] = 0
    hc[:, p, off, t] = 0
    return whole(x.reshape(N, 128, 4 * P), hc.reshape(N, 128, 4 * P), u, d["w"])
def check_inputs(d):
    b = []
    for k, lo, hi in (("x", -16, 24), ("hl", -16, 24), ("hc", -16, 24), ("hr", -16, 24), ("u", -30, 30), ("w", -30, 30)):
        v = np.abs(d[k].astype(np.float32))
        if not (np.isfinite(v).all() and ((v == 0) | (v >= 2.0 ** lo) & (v <= 2.0 ** hi)).all()): b.append("a value of " + k)
    i = np.arange(N)
    hl, hc, hr, u = [d[k].astype(np.float32) for k in ("hl", "hc", "hr", "u")]
    if (hl != hc[(i - 1) % N]).any(): b.append("hl isn't the left neighbour's hc")
    if (hr != hc[(i + 1) % N]).any(): b.append("hr isn't the right neighbour's hc")
    if (u != u[:1]).any(): b.append("u isn't the same on all ranks")
    if (d["u"][:, :, 4:].astype(np.float32) != 0).any(): b.append("u has numbers behind its column 0")
    return b
def reference(x, hl, hc, hr, u, w):
    a, h, b = [[mx_ref.quantize(np.ascontiguousarray(v[r])) for r in range(N)] for v in (hl, hc, hr)]
    s = [x[r] for r in range(N)]
    ch = np.zeros((N, R, K), np.float32)
    for t in range(R):
        dh = decode(join(*h)).reshape(128, N, 4 * P).transpose(1, 0, 2)
        at, dq = [], []
        for r in range(N):
            v = ((dh[(r - 1) % N] + dh[(r + 1) % N]) - dh[r] * np.float32(2)) * np.float32(0.25)
            s[r] = (s[r].astype(np.float32) + v).astype(BF)
            q = mx_ref.quantize(np.ascontiguousarray((s[r].astype(np.float32) - dh[r]).astype(BF)))
            z = np.abs(mx_ref.matmul(mx_ref.quantize(np.ascontiguousarray(u[r])), q)[0]) + np.float32(0)
            e = np.argsort(-z, kind="stable")[:K]
            ch[r, t] = e
            at.append(e)
            dq.append(pick(q, e))
        dd = decode(join(*dq)).reshape(128, N, K, 4)
        for r in range(N):
            v = mx_ref.quantize(np.ascontiguousarray((dh[r].reshape(128, P, 4)[:, at[r]] + dd[:, r]).reshape(128, -1).astype(BF)))
            for held, o in ((a, (r + 1) % N), (h, r), (b, (r - 1) % N)): held[o] = put(held[o], at[r], v)
    oc, osc = np.zeros((N, 128, 12 * P), np.uint8), np.zeros((N, 16, 3 * P), np.uint8)
    y = np.zeros((N, 128, P), np.float32)
    for r in range(N):
        oc[r], osc[r] = emit(join(a[r], h[r], b[r]))
        y[r] = mx_ref.matmul(mx_ref.quantize(np.ascontiguousarray(w[r])), a[r])
    return {"oc": oc, "osc": osc, "xe": np.stack(s).astype(np.float32), "ch": ch, "y": y}

@@ -1,0 +1,291 @@
+from concourse.bass import DstId, RemoteDMATransfer
+from concourse.mybir import dt, AluOpType as OP, AxisListType, ActivationFunctionType as AF
+
+P, K, R = 192, 48, 3
+BF, F32, I32, U16, FP8, U8 = "bfloat16", "float32", "int32", "uint16", "float8_e4m3fn_x4", "uint8"
+SND = P + K + 12
+
+SCRATCH = {}
+SCRATCH.update({n: ("sbuf", [128, w], BF) for n, w in dict(
+    x0=768, x1=768, x2=768, x3=768, tl=768, tc=768, tr=768, tu=4, tw=512, ub=512, ones=128, ident=128, z128=128, stage=2048,
+    cet=512, cst=512, z384=384, thr=384, k96=96, k192=192, dtile=768, stile=768, g0=208, g1=208, junk=208, ot=512,
+    xt=512).items()})
+SCRATCH.update({n: ("sbuf", [128, w], F32) for n, w in dict(
+    lf=1, hf=1, h1=1, jc=2, cz=4, row16=12, bm=12, sab=192, sc0=1, nsc=1, df0=192, df1=192, rr=2, t2=2, vv=2, xf=12, etr=96,
+    chs=R * K, xout=768, yout=192).items()})
+SCRATCH.update({n: ("sbuf", [128, w], I32) for n, w in dict(pint=1, lint=1, am=128, am15=128).items()})
+_Q = dict(uq=128, wq=128, e1=512, eq=512, em=512, ce=128, cs=128, dq=P, oq=128, fin=3 * P)
+for _t in range(R):
+    _Q.update({"wA%d" % _t: SND, "wB%d" % _t: SND, "wH%d" % _t: P + K + 128, "sq%d" % _t: P})
+    SCRATCH["eo%d" % _t] = ("sbuf", [128, 4], U16)
+    for _n in "AHB":
+        SCRATCH["so%s%d" % (_n, _t)] = ("sbuf", [128, 12], U16)
+for _n, _w in _Q.items():
+    SCRATCH[_n] = ("sbuf", [128, _w], FP8)
+    SCRATCH[_n + "_s"] = ("sbuf", [128, _w], U8)
+for _b in range(4):
+    SCRATCH["psZ%d" % _b] = ("psum", [128, 512], F32)
+    SCRATCH["psH%d" % _b] = ("psum", [128, 512], F32)
+
+SEMAPHORES = (["sv", "sa", "st", "sg", "left", "lc", "ll", "lr", "lx", "lu", "lw", "out"]
+              + ["rA%d" % t for t in range(R)] + ["rB%d" % t for t in range(R)])
+
+
+def rank_program(g, core, T, topo):
+    rank = T.rank_of(core)
+    if rank is None:
+        return
+    n = len(T.cores)
+    right, left = T.cores[(rank + 1) % n], T.cores[(rank - 1) % n]
+    Q = {"v": g.vector, "a": g.scalar, "t": g.tensor, "g": g, "s": g.sync}
+    cnt = {"v": 0, "a": 0, "t": 0, "g": 0}
+    seen = {q: {} for q in Q}
+    total = {"out": 0, "left": 0}
+
+    def wait(q, deps):
+        need = {}
+        for s, v in deps:
+            need[s] = max(v, need.get(s, 0))
+        for s, v in need.items():
+            if seen[q].get(s, 0) < v:
+                Q[q].wait_ge(T.sem[s], v)
+                seen[q][s] = v
+
+    CALLS = {"act": g.scalar.activation, "mm": g.tensor.matmul_mx, "quant": g.vector.quantize_mx, "copy": g.vector.tensor_copy,
+             "tt": g.vector.tensor_tensor, "ts": g.vector.tensor_scalar, "red": g.vector.tensor_reduce,
+             "tr": g.vector.transpose, "fill": g.vector.memset, "iota": g.iota, "select": g.affine_select}
+    QUEUE = {"act": "a", "mm": "t", "iota": "g", "select": "g"}
+
+    def run(name, deps, *args, **kw):
+        q = QUEUE.get(name, "v")
+        wait(q, deps)
+        CALLS[name](*args, **kw).then_inc(T.sem["s" + q], 1)
+        cnt[q] += 1
+        return ("s" + q, cnt[q])
+
+    def load(q, sem, out, in_):
+        Q[q].dma_start(out, in_).then_inc(T.sem[sem], 16)
+        return (sem, 16)
+
+    def store(q, deps, out, in_):
+        wait(q, deps)
+        Q[q].dma_start(out, in_).then_inc(T.sem.out, 16)
+        total["out"] += 16
+
+    def ts(deps, out, in0, s1, op0, s2=None, op1=None):
+        kw = {} if op1 is None else {"op1": op1}
+        return run("ts", deps, out=out, in0=in0, scalar1=s1, scalar2=s2, op0=op0, **kw)
+
+    def cols(name, a, b):
+        return T[name][:, a:b], T[name + "_s"][:, a:b]
+
+    def win(k, t, a, b):
+        o = P * "AHB".index(k)
+        return cols("fin", o + a, o + b) if t == R else cols("w%s%d" % (k, t), a, b)
+
+    def mm(deps, out, l, r, start=True, stop=True):
+        return run("mm", deps, out, l[0], l[1], r[0], r[1], start, stop)
+
+    def quant(deps, q, tile):
+        return run("quant", deps, q[0], q[1], tile)
+
+    psZ = [T["psZ%d" % b] for b in range(4)]
+    psH = [T["psH%d" % b] for b in range(4)]
+    XS = [T.x0, T.x1, T.x2, T.x3]
+    U, DQ, CE, CS, OQ = cols("uq", 0, 128), cols("dq", 0, P), cols("ce", 0, 128), cols("cs", 0, 128), cols("oq", 0, 128)
+    E = {c: [cols(c, 128 * b, 128 * b + 128) for b in range(4)] for c in ("e1", "eq", "em")}
+
+    lc = load("s", "lc", T.tc[:], T.hc[:])
+    ll = load("a", "ll", T.tl[:], T.hl[:])
+    lr = load("s", "lr", T.tr[:], T.hr[:])
+    lx = load("a", "lx", T.x0[:], T.x[:])
+    lu = load("s", "lu", T.tu[:], T.u[:, 0:4])
+    lw = load("s", "lw", T.tw[:], T.w[:])
+
+    c_ones = run("fill", [], T.ones[:], 1.0)
+    c_id = run("select", [c_ones], T.ident[:], T.ones[:], [[-1, 128]], OP.is_equal, 0.0, 0, 1)
+    c_z = run("fill", [], T.z128[:], 0.0)
+    c_stage = run("fill", [], T.stage[:], 0.0)
+    c_z384 = run("fill", [], T.z384[:], 0.0)
+    small = {"allow_small_or_imprecise_dtypes": True}
+    i_p = run("iota", [], T.pint[:], [[0, 1]], 0, 1)
+    i_am = run("iota", [], T.am[:], [[1, 128]], 128, -1)
+    i_k = run("iota", [], T.k96[:], [[16, 3], [0, 2], [1, 16]], P, 0, **small)
+    i_r = run("iota", [], T.row16[:], [[16, 12]], 0, 0, **small)
+    i_t = run("select", [c_z384], T.thr[:], T.z384[:], [[-64, 2], [1, P]], OP.is_ge, -(2.0 ** -120), 0, -1)
+
+    def const(c, name, before):
+        d = [ts([c_id, c_stage] + before, T.stage[:, 512 * b + b:512 * (b + 1):4], T.ident[:], c, OP.mult) for b in range(4)]
+        return quant(d, cols(name, 0, 512), T.stage[:])
+
+    u4 = [run("act", [lu, c_z], T.ub[:, t:512:4], T.z128[:], AF.Identity, bias=T.tu[:, t:t + 1]) for t in range(4)]
+    k_e1 = const(1.0, "e1", [])
+    k_eq = const(0.25, "eq", [k_e1])
+    sh = {"H": [quant([lc], win("H", 0, 0, P), T.tc[:])], "A": [quant([ll], win("A", 0, 0, P), T.tl[:])]}
+    k_em = const(-0.5, "em", [k_eq])
+    sh["B"] = [quant([lr], win("B", 0, 0, P), T.tr[:])]
+
+    free = {(k, b): [] for b in range(4) for k in "ZH"}
+
+    def decode_h(t):
+        return [mm(sh["H"] + free["H", b] + [k_e1], psH[b][:, 0:P], E["e1"][b], win("H", t, 0, P)) for b in range(4)]
+
+    def decode_z(t):
+        for b in range(4):
+            mm(sh["A"] + free["Z", b] + [k_eq], psZ[b][:, 0:P], E["eq"][b], win("A", t, 0, P), True, False)
+        z = []
+        for b in range(4):
+            mm(sh["B"], psZ[b][:, 0:P], E["eq"][b], win("B", t, 0, P), False, False)
+            z.append(mm([k_em], psZ[b][:, 0:P], E["em"][b], win("H", t, 0, P), False, True))
+        return z
+
+    tH = decode_h(0)
+    tZ = decode_z(0)
+
+    k_u = quant(u4, U, T.ub[:])
+    v_l = ts([i_p], T.lint[:], T.pint[:], 15, OP.bitwise_and)
+    v_j = run("copy", [i_p], T.jc[:, 0:1], T.pint[:])
+    v_am = ts([i_am], T.am15[:], T.am[:], 15, OP.bitwise_and)
+    v_lf = run("copy", [v_l], T.lf[:], T.lint[:])
+    v_j1 = ts([v_j], T.jc[:, 1:2], T.jc[:, 0:1], 64.0, OP.add)
+    v_cs0 = run("fill", [], T.cst[:], 0.0)
+    v_hf = run("tt", [v_lf, v_j], T.hf[:], T.jc[:, 0:1], T.lf[:], OP.subtract)
+    v_cz = run("fill", [], T.cz[:], 0.0)
+    v_c = [ts([v_am, v_cs0], T.cst[:, t:512:4], T.am15[:], 0.0, OP.is_equal) for t in range(2)]
+    v_h1 = ts([v_hf], T.h1[:], T.hf[:], 64.0, OP.add)
+    v_z = [run("copy", [v_cz, v_hf], T.cz[:, 0:1], T.hf[:]),
+           run("copy", [v_cz, v_lf], T.cz[:, 2:3], T.lf[:]),
+           run("copy", [v_cz, v_lf], T.cz[64:128, 3:4], T.lf[64:128, :]),
+           run("copy", [v_cz, v_h1], T.cz[64:128, 1:2], T.h1[64:128, :])]
+    k_cs = quant(v_c, CS, T.cst[:])
+    v_e = [run("act", [c_z] + v_z, T.cet[:, t:512:4], T.z128[:], AF.Identity, bias=T.cz[:, t:t + 1]) for t in range(4)]
+    v_b0 = ts([i_r, v_hf], T.bm[:, 0:8], T.row16[:, 0:8], T.hf[:], OP.is_equal)
+    v_b1 = ts([i_r, v_h1], T.bm[:, 8:12], T.row16[:, 8:12], T.h1[:], OP.is_equal)
+    v_k = [run("copy", [i_k], T.k192[:, t:192:2], T.k96[:]) for t in range(2)]
+    v_f = [run("fill", [], T.g0[:, P:P + 16], float(P)), run("fill", [], T.g1[:, P:P + 16], float(P)),
+           run("fill", [], T.ot[:, 384:512], 0.0), run("fill", [], T.xt[:], 0.0)]
+    k_ce, k_w = [], []
+
+    def send(deps, src, to_right, to_left, t):
+        wait("g", deps)
+        tr = []
+        for who, dst, sem, odd in ((right, to_right, "rA%d" % t, 0), (left, to_left, "rB%d" % t, 1)):
+            rid, pid, _ = topo.addr(who)
+            eng = topo.engines(core, who)[odd::2]
+            tr.append(RemoteDMATransfer(dst_ids=[DstId(rid=rid, pnc=pid)], dma_engine_mask=sum(1 << e for e in eng),
+                                        remote_sem=T.sem[sem], src=src, dst=dst))
+            total["left"] += len(eng)
+        g.remote_dma_fused(tr, local_sem=T.sem.left)
+
+    got = {"A": 2 * len(topo.engines(left, core)[0::2]), "B": 2 * len(topo.engines(right, core)[1::2])}
+    chtok = []
+
+    for t in range(R):
+        last = t == R - 1
+        tx, td = [], []
+
+        def state(b):
+            e = slice(b, 4 * P, 4)
+            tx.append(run("tt", [tZ[b], lx], XS[t + 1][:, e], psZ[b][:, 0:P], XS[t][:, e], OP.add))
+
+        def drift(b):
+            e = slice(b, 4 * P, 4)
+            td.append(run("tt", [tx[b], tH[b]], T.dtile[:, e], XS[t + 1][:, e], psH[b][:, 0:P], OP.subtract))
+
+        state(0)
+        for b in range(1, 4):
+            state(b)
+            drift(b - 1)
+        drift(3)
+        tq = quant(td, DQ, T.dtile[:])
+        for b in range(4):
+            mm([tx[b]], psZ[b][:, 0:P], E["e1"][b], win("H", t, 0, P), True, False)
+        mr = mm([tq, k_u], psH[0][:, 0:P], U, DQ)
+        mc0 = mm([tq], psH[1][:, 0:128], cols("dq", 0, 128), U)
+        mc1 = mm([tq], psH[2][:, 0:128], cols("dq", 64, 192), U)
+        mS = [mm([tq], psZ[b][:, 0:P], E["e1"][b], DQ, False, True) for b in range(4)]
+
+        def candidate(b):
+            return run("act", [mS[b]], T.stile[:, b:4 * P:4], psZ[b][:, 0:P], AF.Copy)
+
+        aA = run("act", [mr], T.sab[:], psH[0][:, 0:P], AF.Abs)
+        vc0 = run("red", [mc0], T.sc0[:], psH[1][:, 0:2], AxisListType.X, OP.max, negate=False, apply_absolute_value=True)
+        vc1 = run("red", [mc1], T.nsc[:], psH[2][:, 0:2], AxisListType.X, OP.max, negate=True, apply_absolute_value=True)
+        vd0 = ts([aA, vc0], T.df0[:], T.sab[:], T.sc0[:], OP.subtract)
+        ad1 = run("act", [aA, vc1], T.df1[:], T.sab[:], AF.Identity, bias=T.nsc[:])
+        vg0 = run("tt", [vd0, i_t], T.g0[:, 0:P], T.df0[:], T.thr[:, 0:P], OP.is_gt)
+        vg1 = run("tt", [ad1, i_t], T.g1[:, 0:P], T.df1[:], T.thr[:, P:2 * P], OP.is_gt)
+        aS = [candidate(0)]
+        ar0 = run("act", [vg0] + v_f, T.junk[:, 0:P + 1], T.g0[:, 0:P + 1], AF.Copy, accum_out=T.rr[:, 0:1])
+        aS += [candidate(b) for b in range(1, 4)]
+        vo0 = ts([ar0] + v_k, T.ot[:, 0:384:2], T.k192[:], T.rr[:, 0:1], OP.is_equal)
+        vr1 = run("red", [vg1] + v_f, T.rr[:, 1:2], T.g1[:, 0:P + 1], AxisListType.X, OP.add)
+        vo1 = ts([vr1] + v_k, T.ot[:, 1:384:2], T.k192[:], T.rr[:, 1:2], OP.is_equal)
+        if t == 0:
+            k_ce.append(quant(v_e, CE, T.cet[:]))
+        vqo = quant([vo0, vo1], OQ, T.ot[:])
+        me = mm([vqo] + k_ce, psH[3][:, 0:128], CE, OQ)
+        S, eo = cols("sq%d" % t, 0, P), T["eo%d" % t]
+        v2 = ts([ar0, vr1], T.t2[:], T.rr[:], -512.0, OP.mult, 122608.0, OP.add)
+        vqs = quant(aS, S, T.stile[:])
+        vv = [ts([v2, v_j1], T.vv[:, h:h + 1], T.rr[:, h:h + 1], T.t2[:, h:h + 1], OP.min, T.jc[:, h:h + 1], OP.max)
+              for h in range(2)]
+        ve = run("tr", [me], T.etr[:], psH[3][:, 0:96])
+        vx = [ts([vv[0], v_b0], T.xf[:, 0:8], T.bm[:, 0:8], T.vv[:, 0:1], OP.mult),
+              ts([vv[1], v_b1], T.xf[:, 8:12], T.bm[:, 8:12], T.vv[:, 1:2], OP.mult)]
+        veo = run("copy", [ve], eo[:, 0:3], T.etr[:, 0:96:32])
+        big = 1.5 * 2.0 ** 27
+        vh = ts(vx, T.xt[:, 0:48:4], T.xf[:], big, OP.add, big, OP.subtract)
+        H, X, msg = win("H", t, P, P + K), win("H", t, P + K, P + K + 128), win("H", t, P, SND)
+        vp = run("copy", [veo, vqs], H[0].bitcast(dt.uint32), S[0].bitcast(dt.uint32).indirect(eo[:, 0:3]))
+        ap = run("act", [veo, vqs], H[1], S[1].indirect(eo[:, 0:3]), AF.Copy)
+        vl = run("tt", [vh], T.xt[:, 1:48:4], T.xf[:], T.xt[:, 0:48:4], OP.subtract)
+        vqx = quant([vl, vh], X, T.xt[:])
+        da, db = win("A", t, P, SND), win("B", t, P, SND)
+        send([vp, vqx], msg[0].bitcast(dt.uint8), da[0].bitcast(dt.uint8), db[0].bitcast(dt.uint8), t)
+        send([ap, vqx], msg[1], da[1], db[1], t)
+        ach = [run("act", [ve], T.chs[0:1, K * t + 16 * m:K * t + 16 * m + 16], psH[3][0:1, 32 * m:32 * m + 16], AF.Copy)
+               for m in range(3)]
+        chtok.append(ach[-1])
+
+        def places(k, deps, bank, tile, c):
+            m = mm(deps + [k_cs], bank[:, 0:128], CS, tile)
+            return run("copy", [m], T["so%s%d" % (k, t)][:], bank[:, c:c + 12])
+
+        def pick(k, deps):
+            so, d, w = T["so%s%d" % (k, t)], win(k, t + 1, 0, P), cols("w%s%d" % (k, t), 0, SND)
+            return [run("copy", deps, d[0].bitcast(dt.uint32), w[0].bitcast(dt.uint32).indirect(so[:])),
+                    run("act", deps, d[1], w[1].indirect(so[:]), AF.Copy)]
+
+        vsh = places("H", [vqx, aS[0]], psZ[0], X, 0)
+        sh["H"] = pick("H", [vsh, vp, ap])
+        for b, d in enumerate(([aA], [vc0], [vc1], ach + [ve])):
+            free["H", b] = d
+        if not last:
+            tH = decode_h(t + 1)
+        else:
+            k_w.append(quant([lw], cols("wq", 0, 128), T.tw[:]))
+            axo = run("act", tx, T.xout[:], XS[R][:], AF.Copy)
+            store("s", [axo], T.xe[:], T.xout[:])
+            store("s", chtok, T.ch[:], T.chs[0:1, :])
+            store("s", sh["H"], T.oc[:, 4 * P:8 * P], T.fin[:, P:2 * P].bitcast(dt.uint8))
+        ra, rb = ("rA%d" % t, got["A"]), ("rB%d" % t, got["B"])
+        ma = mm([ra, aS[2], k_cs], psZ[2][:, 0:128], CS, win("A", t, SND - 128, SND))
+        mb = mm([rb, aS[3]], psZ[3][:, 0:128], CS, win("B", t, SND - 128, SND))
+        vsa = run("copy", [ma], T["soA%d" % t][:], psZ[2][:, 116:128])
+        vsb = run("copy", [mb], T["soB%d" % t][:], psZ[3][:, 116:128])
+        sh["A"] = pick("A", [vsa, ra])
+        sh["B"] = pick("B", [vsb, rb])
+        for b, d in enumerate((vsh, aS[1], vsa, vsb)):
+            free["Z", b] = [d]
+        if not last:
+            tZ = decode_z(t + 1)
+
+    my = mm(sh["A"] + free["Z", 0] + k_w, psZ[0][:, 0:P], cols("wq", 0, 128), win("A", R, 0, P))
+    vy = run("copy", [my], T.yout[:], psZ[0][:, 0:P])
+    store("s", sh["A"], T.oc[:, 0:4 * P], T.fin[:, 0:P].bitcast(dt.uint8))
+    store("s", sh["B"], T.oc[:, 8 * P:12 * P], T.fin[:, 2 * P:3 * P].bitcast(dt.uint8))
+    for k in range(4):
+        store("a" if k % 2 else "s", sh["A"] + sh["B"] + sh["H"], T.osc[4 * k:4 * k + 4, :], T.fin_s[32 * k:32 * k + 4, :])
+    store("a", [vy], T.y[:], T.yout[:])
+    wait("g", [("s" + q, c) for q, c in cnt.items()] + list(total.items()))

@@ -4,14 +4,14 @@ from concourse.mybir import dt, AluOpType as OP, AxisListType, ActivationFunctio
 P, K, R = 192, 48, 3
 BF, F32, I32, U16, FP8, U8 = "bfloat16", "float32", "int32", "uint16", "float8_e4m3fn_x4", "uint8"
 SND = P + K + 12
+STEPS = "x0 x1 d0 x2 d1 x3 d2 d3"
 
 SCRATCH = {}
 SCRATCH.update({n: ("sbuf", [128, w], BF) for n, w in dict(
     x0=768, x1=768, x2=768, x3=768, tl=768, tc=768, tr=768, tu=4, tw=512, ub=512, ones=128, ident=128, z128=128, stage=2048,
-    cet=512, cst=512, z384=384, thr=384, k96=96, k192=192, dtile=768, stile=768, g0=208, g1=208, junk=208, ot=512,
-    xt=512).items()})
+    cet=512, cst=512, thr=192, k96=96, k192=192, dtile=768, stile=768, g0=208, g1=208, ot=512, xt=512).items()})
 SCRATCH.update({n: ("sbuf", [128, w], F32) for n, w in dict(
-    lf=1, hf=1, h1=1, jc=2, cz=4, row16=12, bm=12, sab=192, sc0=1, nsc=1, df0=192, df1=192, rr=2, t2=2, vv=2, xf=12, etr=96,
+    lf=1, hf=1, h1=1, jc=2, cz=4, row16=12, bm=12, sab=192, nsc=2, df=192, rr=2, t2=2, vv=2, xf=12, etr=96,
     chs=R * K, xout=768, yout=192).items()})
 SCRATCH.update({n: ("sbuf", [128, w], I32) for n, w in dict(pint=1, lint=1, am=128, am15=128).items()})
 _Q = dict(uq=128, wq=128, e1=512, eq=512, em=512, ce=128, cs=128, dq=P, oq=128, fin=3 * P)
@@ -94,25 +94,27 @@ def rank_program(g, core, T, topo):
     XS = [T.x0, T.x1, T.x2, T.x3]
     U, DQ, CE, CS, OQ = cols("uq", 0, 128), cols("dq", 0, P), cols("ce", 0, 128), cols("cs", 0, 128), cols("oq", 0, 128)
     E = {c: [cols(c, 128 * b, 128 * b + 128) for b in range(4)] for c in ("e1", "eq", "em")}
+    row = [slice(b, 4 * P, 4) for b in range(4)]
 
     lc = load("s", "lc", T.tc[:], T.hc[:])
     ll = load("a", "ll", T.tl[:], T.hl[:])
+    lu = load("s", "lu", T.tu[:], T.u[:, 0:4])
     lr = load("s", "lr", T.tr[:], T.hr[:])
     lx = load("a", "lx", T.x0[:], T.x[:])
-    lu = load("s", "lu", T.tu[:], T.u[:, 0:4])
     lw = load("s", "lw", T.tw[:], T.w[:])
 
     c_ones = run("fill", [], T.ones[:], 1.0)
     c_id = run("select", [c_ones], T.ident[:], T.ones[:], [[-1, 128]], OP.is_equal, 0.0, 0, 1)
     c_z = run("fill", [], T.z128[:], 0.0)
     c_stage = run("fill", [], T.stage[:], 0.0)
-    c_z384 = run("fill", [], T.z384[:], 0.0)
     small = {"allow_small_or_imprecise_dtypes": True}
     i_p = run("iota", [], T.pint[:], [[0, 1]], 0, 1)
     i_am = run("iota", [], T.am[:], [[1, 128]], 128, -1)
     i_k = run("iota", [], T.k96[:], [[16, 3], [0, 2], [1, 16]], P, 0, **small)
     i_r = run("iota", [], T.row16[:], [[16, 12]], 0, 0, **small)
-    i_t = run("select", [c_z384], T.thr[:], T.z384[:], [[-64, 2], [1, P]], OP.is_ge, -(2.0 ** -120), 0, -1)
+    tiny = -(2.0 ** -120)
+    i_t0 = run("select", [c_z], T.thr[:, 0:128], T.z128[:], [[1, 128]], OP.is_ge, tiny, 0, -1)
+    i_t1 = run("select", [c_z], T.thr[:, 128:P], T.z128[:, 0:64], [[1, 64]], OP.is_ge, tiny, 64, -1)
 
     def const(c, name, before):
         d = [ts([c_id, c_stage] + before, T.stage[:, 512 * b + b:512 * (b + 1):4], T.ident[:], c, OP.mult) for b in range(4)]
@@ -121,8 +123,8 @@ def rank_program(g, core, T, topo):
     u4 = [run("act", [lu, c_z], T.ub[:, t:512:4], T.z128[:], AF.Identity, bias=T.tu[:, t:t + 1]) for t in range(4)]
     k_e1 = const(1.0, "e1", [])
     k_eq = const(0.25, "eq", [k_e1])
-    sh = {"H": [quant([lc], win("H", 0, 0, P), T.tc[:])], "A": [quant([ll], win("A", 0, 0, P), T.tl[:])]}
     k_em = const(-0.5, "em", [k_eq])
+    sh = {"H": [quant([lc], win("H", 0, 0, P), T.tc[:])], "A": [quant([ll], win("A", 0, 0, P), T.tl[:])]}
     sh["B"] = [quant([lr], win("B", 0, 0, P), T.tr[:])]
 
     free = {(k, b): [] for b in range(4) for k in "ZH"}
@@ -131,9 +133,9 @@ def rank_program(g, core, T, topo):
         return [mm(sh["H"] + free["H", b] + [k_e1], psH[b][:, 0:P], E["e1"][b], win("H", t, 0, P)) for b in range(4)]
 
     def decode_z(t):
+        z = []
         for b in range(4):
             mm(sh["A"] + free["Z", b] + [k_eq], psZ[b][:, 0:P], E["eq"][b], win("A", t, 0, P), True, False)
-        z = []
         for b in range(4):
             mm(sh["B"], psZ[b][:, 0:P], E["eq"][b], win("B", t, 0, P), False, False)
             z.append(mm([k_em], psZ[b][:, 0:P], E["em"][b], win("H", t, 0, P), False, True))
@@ -182,22 +184,15 @@ def rank_program(g, core, T, topo):
 
     for t in range(R):
         last = t == R - 1
-        tx, td = [], []
-
-        def state(b):
-            e = slice(b, 4 * P, 4)
-            tx.append(run("tt", [tZ[b], lx], XS[t + 1][:, e], psZ[b][:, 0:P], XS[t][:, e], OP.add))
-
-        def drift(b):
-            e = slice(b, 4 * P, 4)
-            td.append(run("tt", [tx[b], tH[b]], T.dtile[:, e], XS[t + 1][:, e], psH[b][:, 0:P], OP.subtract))
-
-        state(0)
-        for b in range(1, 4):
-            state(b)
-            drift(b - 1)
-        drift(3)
-        tq = quant(td, DQ, T.dtile[:])
+        tx, td = {}, {}
+        for step in STEPS.split():
+            b = int(step[1])
+            x = XS[t + 1][:, row[b]]
+            if step[0] == "x":
+                tx[b] = run("tt", [tZ[b], lx], x, psZ[b][:, 0:P], XS[t][:, row[b]], OP.add)
+            else:
+                td[b] = run("tt", [tx[b], tH[b]], T.dtile[:, row[b]], x, psH[b][:, 0:P], OP.subtract)
+        tq = quant(list(td.values()), DQ, T.dtile[:])
         for b in range(4):
             mm([tx[b]], psZ[b][:, 0:P], E["e1"][b], win("H", t, 0, P), True, False)
         mr = mm([tq, k_u], psH[0][:, 0:P], U, DQ)
@@ -205,41 +200,44 @@ def rank_program(g, core, T, topo):
         mc1 = mm([tq], psH[2][:, 0:128], cols("dq", 64, 192), U)
         mS = [mm([tq], psZ[b][:, 0:P], E["e1"][b], DQ, False, True) for b in range(4)]
 
-        def candidate(b):
-            return run("act", [mS[b]], T.stile[:, b:4 * P:4], psZ[b][:, 0:P], AF.Copy)
+        def minus(m, bank, h):
+            return run("red", [m], T.nsc[:, h:h + 1], bank[:, 0:2], AxisListType.X, OP.max, negate=True,
+                       apply_absolute_value=True)
 
+        n0, n1 = T.nsc[:, 0:1], T.nsc[:, 1:2]
         aA = run("act", [mr], T.sab[:], psH[0][:, 0:P], AF.Abs)
-        vc0 = run("red", [mc0], T.sc0[:], psH[1][:, 0:2], AxisListType.X, OP.max, negate=False, apply_absolute_value=True)
-        vc1 = run("red", [mc1], T.nsc[:], psH[2][:, 0:2], AxisListType.X, OP.max, negate=True, apply_absolute_value=True)
-        vd0 = ts([aA, vc0], T.df0[:], T.sab[:], T.sc0[:], OP.subtract)
-        ad1 = run("act", [aA, vc1], T.df1[:], T.sab[:], AF.Identity, bias=T.nsc[:])
-        vg0 = run("tt", [vd0, i_t], T.g0[:, 0:P], T.df0[:], T.thr[:, 0:P], OP.is_gt)
-        vg1 = run("tt", [ad1, i_t], T.g1[:, 0:P], T.df1[:], T.thr[:, P:2 * P], OP.is_gt)
-        aS = [candidate(0)]
-        ar0 = run("act", [vg0] + v_f, T.junk[:, 0:P + 1], T.g0[:, 0:P + 1], AF.Copy, accum_out=T.rr[:, 0:1])
-        aS += [candidate(b) for b in range(1, 4)]
-        vo0 = ts([ar0] + v_k, T.ot[:, 0:384:2], T.k192[:], T.rr[:, 0:1], OP.is_equal)
-        vr1 = run("red", [vg1] + v_f, T.rr[:, 1:2], T.g1[:, 0:P + 1], AxisListType.X, OP.add)
-        vo1 = ts([vr1] + v_k, T.ot[:, 1:384:2], T.k192[:], T.rr[:, 1:2], OP.is_equal)
+        aS = [run("act", [mS[b]], T.stile[:, row[b]], psZ[b][:, 0:P], AF.Copy) for b in range(4)]
+        vc0 = minus(mc0, psH[1], 0)
+        vc1 = minus(mc1, psH[2], 1)
+        vd0 = ts([aA, vc0], T.df[:, 0:128], T.sab[:, 0:128], n0, OP.add)
+        vd1 = ts([aA, vc1], T.df[:, 128:P], T.sab[:, 128:P], n1, OP.add)
+        vi0 = ts([aA, vc0], T.g0[:, 128:P], T.sab[:, 128:P], n0, OP.add, 0.0, OP.is_gt)
+        vg0 = run("tt", [vd0, i_t0], T.g0[:, 0:128], T.df[:, 0:128], T.thr[:, 0:128], OP.is_gt)
+        vg1 = run("tt", [vd1, i_t1], T.g1[:, 128:P], T.df[:, 128:P], T.thr[:, 128:P], OP.is_gt)
+        vi1 = ts([aA, vc1], T.g1[:, 0:128], T.sab[:, 0:128], n1, OP.add, 0.0, OP.is_ge)
         if t == 0:
             k_ce.append(quant(v_e, CE, T.cet[:]))
+        vr0 = run("red", [vg0, vi0] + v_f, T.rr[:, 0:1], T.g0[:, 0:P + 1], AxisListType.X, OP.add)
+        vr1 = run("red", [vg1, vi1] + v_f, T.rr[:, 1:2], T.g1[:, 0:P + 1], AxisListType.X, OP.add)
+        vo0 = ts([vr0] + v_k, T.ot[:, 0:384:2], T.k192[:], T.rr[:, 0:1], OP.is_equal)
+        vo1 = ts([vr1] + v_k, T.ot[:, 1:384:2], T.k192[:], T.rr[:, 1:2], OP.is_equal)
+        v2 = ts([vr0, vr1], T.t2[:], T.rr[:], -512.0, OP.mult, 122608.0, OP.add)
         vqo = quant([vo0, vo1], OQ, T.ot[:])
         me = mm([vqo] + k_ce, psH[3][:, 0:128], CE, OQ)
         S, eo = cols("sq%d" % t, 0, P), T["eo%d" % t]
-        v2 = ts([ar0, vr1], T.t2[:], T.rr[:], -512.0, OP.mult, 122608.0, OP.add)
-        vqs = quant(aS, S, T.stile[:])
         vv = [ts([v2, v_j1], T.vv[:, h:h + 1], T.rr[:, h:h + 1], T.t2[:, h:h + 1], OP.min, T.jc[:, h:h + 1], OP.max)
               for h in range(2)]
+        vqs = quant(aS, S, T.stile[:])
+        vx = [ts([vv[h], v_b0, v_b1], T.xf[:, c:d], T.bm[:, c:d], T.vv[:, h:h + 1], OP.mult)
+              for h, c, d in ((0, 0, 8), (1, 8, 12))]
         ve = run("tr", [me], T.etr[:], psH[3][:, 0:96])
-        vx = [ts([vv[0], v_b0], T.xf[:, 0:8], T.bm[:, 0:8], T.vv[:, 0:1], OP.mult),
-              ts([vv[1], v_b1], T.xf[:, 8:12], T.bm[:, 8:12], T.vv[:, 1:2], OP.mult)]
-        veo = run("copy", [ve], eo[:, 0:3], T.etr[:, 0:96:32])
         big = 1.5 * 2.0 ** 27
         vh = ts(vx, T.xt[:, 0:48:4], T.xf[:], big, OP.add, big, OP.subtract)
+        veo = run("copy", [ve], eo[:, 0:3], T.etr[:, 0:96:32])
+        vl = run("tt", [vh], T.xt[:, 1:48:4], T.xf[:], T.xt[:, 0:48:4], OP.subtract)
         H, X, msg = win("H", t, P, P + K), win("H", t, P + K, P + K + 128), win("H", t, P, SND)
         vp = run("copy", [veo, vqs], H[0].bitcast(dt.uint32), S[0].bitcast(dt.uint32).indirect(eo[:, 0:3]))
         ap = run("act", [veo, vqs], H[1], S[1].indirect(eo[:, 0:3]), AF.Copy)
-        vl = run("tt", [vh], T.xt[:, 1:48:4], T.xf[:], T.xt[:, 0:48:4], OP.subtract)
         vqx = quant([vl, vh], X, T.xt[:])
         da, db = win("A", t, P, SND), win("B", t, P, SND)
         send([vp, vqx], msg[0].bitcast(dt.uint8), da[0].bitcast(dt.uint8), db[0].bitcast(dt.uint8), t)
@@ -250,14 +248,14 @@ def rank_program(g, core, T, topo):
 
         def places(k, deps, bank, tile, c):
             m = mm(deps + [k_cs], bank[:, 0:128], CS, tile)
-            return run("copy", [m], T["so%s%d" % (k, t)][:], bank[:, c:c + 12])
+            return lambda: run("copy", [m], T["so%s%d" % (k, t)][:], bank[:, c:c + 12])
 
         def pick(k, deps):
             so, d, w = T["so%s%d" % (k, t)], win(k, t + 1, 0, P), cols("w%s%d" % (k, t), 0, SND)
             return [run("copy", deps, d[0].bitcast(dt.uint32), w[0].bitcast(dt.uint32).indirect(so[:])),
                     run("act", deps, d[1], w[1].indirect(so[:]), AF.Copy)]
 
-        vsh = places("H", [vqx, aS[0]], psZ[0], X, 0)
+        vsh = places("H", [vqx, aS[0]], psZ[0], X, 0)()
         sh["H"] = pick("H", [vsh, vp, ap])
         for b, d in enumerate(([aA], [vc0], [vc1], ach + [ve])):
             free["H", b] = d
@@ -265,16 +263,16 @@ def rank_program(g, core, T, topo):
             tH = decode_h(t + 1)
         else:
             k_w.append(quant([lw], cols("wq", 0, 128), T.tw[:]))
-            axo = run("act", tx, T.xout[:], XS[R][:], AF.Copy)
+            axo = run("act", list(tx.values()), T.xout[:], XS[R][:], AF.Copy)
             store("s", [axo], T.xe[:], T.xout[:])
             store("s", chtok, T.ch[:], T.chs[0:1, :])
             store("s", sh["H"], T.oc[:, 4 * P:8 * P], T.fin[:, P:2 * P].bitcast(dt.uint8))
         ra, rb = ("rA%d" % t, got["A"]), ("rB%d" % t, got["B"])
-        ma = mm([ra, aS[2], k_cs], psZ[2][:, 0:128], CS, win("A", t, SND - 128, SND))
-        mb = mm([rb, aS[3]], psZ[3][:, 0:128], CS, win("B", t, SND - 128, SND))
-        vsa = run("copy", [ma], T["soA%d" % t][:], psZ[2][:, 116:128])
-        vsb = run("copy", [mb], T["soB%d" % t][:], psZ[3][:, 116:128])
+        la = places("A", [ra, aS[2]], psZ[2], win("A", t, SND - 128, SND), 116)
+        lb = places("B", [rb, aS[3]], psZ[3], win("B", t, SND - 128, SND), 116)
+        vsa = la()
         sh["A"] = pick("A", [vsa, ra])
+        vsb = lb()
         sh["B"] = pick("B", [vsb, rb])
         for b, d in enumerate((vsh, aS[1], vsa, vsb)):
             free["Z", b] = [d]

@@ -11,7 +11,7 @@ SCRATCH.update({n: ("sbuf", [128, w], BF) for n, w in dict(
     x0=768, x1=768, x2=768, x3=768, tl=768, tc=768, tr=768, tu=4, tw=512, ub=512, ones=128, ident=128, z128=128, stage=2048,
     cet=512, cst=512, thr=192, k96=96, k192=192, dtile=768, stile=768, g0=208, g1=208, ot=512, xt=512).items()})
 SCRATCH.update({n: ("sbuf", [128, w], F32) for n, w in dict(
-    lf=1, hf=1, h1=1, jc=2, cz=4, row16=12, bm=12, sab=192, nsc=2, df=192, rr=2, t2=2, vv=2, xf=12, etr=96,
+    lf=1, hf=1, h1=1, jc=1, cz=4, row16=12, bm=12, below=12, above=12, sab=192, nsc=2, df=192, rr=2, xf=12, etr=96,
     chs=R * K, xout=768, yout=192).items()})
 SCRATCH.update({n: ("sbuf", [128, w], I32) for n, w in dict(pint=1, lint=1, am=128, am15=128).items()})
 _Q = dict(uq=128, wq=128, e1=512, eq=512, em=512, ce=128, cs=128, dq=P, oq=128, fin=3 * P)
@@ -96,19 +96,19 @@ def rank_program(g, core, T, topo):
     E = {c: [cols(c, 128 * b, 128 * b + 128) for b in range(4)] for c in ("e1", "eq", "em")}
     row = [slice(b, 4 * P, 4) for b in range(4)]
 
-    lc = load("s", "lc", T.tc[:], T.hc[:])
     ll = load("a", "ll", T.tl[:], T.hl[:])
+    lc = load("s", "lc", T.tc[:], T.hc[:])
     lu = load("s", "lu", T.tu[:], T.u[:, 0:4])
     lr = load("s", "lr", T.tr[:], T.hr[:])
     lx = load("a", "lx", T.x0[:], T.x[:])
     lw = load("s", "lw", T.tw[:], T.w[:])
 
-    c_ones = run("fill", [], T.ones[:], 1.0)
-    c_id = run("select", [c_ones], T.ident[:], T.ones[:], [[-1, 128]], OP.is_equal, 0.0, 0, 1)
-    c_z = run("fill", [], T.z128[:], 0.0)
-    c_stage = run("fill", [], T.stage[:], 0.0)
     small = {"allow_small_or_imprecise_dtypes": True}
+    c_ones = run("fill", [], T.ones[:], 1.0)
     i_p = run("iota", [], T.pint[:], [[0, 1]], 0, 1)
+    c_id = run("select", [c_ones], T.ident[:], T.ones[:], [[-1, 128]], OP.is_equal, 0.0, 0, 1)
+    c_stage = run("fill", [], T.stage[:], 0.0)
+    c_z = run("fill", [], T.z128[:], 0.0)
     i_am = run("iota", [], T.am[:], [[1, 128]], 128, -1)
     i_k = run("iota", [], T.k96[:], [[16, 3], [0, 2], [1, 16]], P, 0, **small)
     i_r = run("iota", [], T.row16[:], [[16, 12]], 0, 0, **small)
@@ -116,57 +116,54 @@ def rank_program(g, core, T, topo):
     i_t0 = run("select", [c_z], T.thr[:, 0:128], T.z128[:], [[1, 128]], OP.is_ge, tiny, 0, -1)
     i_t1 = run("select", [c_z], T.thr[:, 128:P], T.z128[:, 0:64], [[1, 64]], OP.is_ge, tiny, 64, -1)
 
-    def const(c, name, before):
-        d = [ts([c_id, c_stage] + before, T.stage[:, 512 * b + b:512 * (b + 1):4], T.ident[:], c, OP.mult) for b in range(4)]
+    def diag(c, before):
+        return [ts([c_id, c_stage] + before, T.stage[:, 512 * b + b:512 * (b + 1):4], T.ident[:], c, OP.mult) for b in range(4)]
+
+    def pack(name, d):
         return quant(d, cols(name, 0, 512), T.stage[:])
 
     u4 = [run("act", [lu, c_z], T.ub[:, t:512:4], T.z128[:], AF.Identity, bias=T.tu[:, t:t + 1]) for t in range(4)]
-    k_e1 = const(1.0, "e1", [])
-    k_eq = const(0.25, "eq", [k_e1])
-    k_em = const(-0.5, "em", [k_eq])
-    sh = {"H": [quant([lc], win("H", 0, 0, P), T.tc[:])], "A": [quant([ll], win("A", 0, 0, P), T.tl[:])]}
+    d = diag(0.25, [])
+    v_l = ts([i_p], T.lint[:], T.pint[:], 15, OP.bitwise_and)
+    v_j = run("copy", [i_p], T.jc[:], T.pint[:])
+    v_cz = run("fill", [], T.cz[:], 0.0)
+    k_eq = pack("eq", d)
+    v_lf = run("copy", [v_l], T.lf[:], T.lint[:])
+    v_am = ts([i_am], T.am15[:], T.am[:], 15, OP.bitwise_and)
+    d = diag(1.0, [k_eq])
+    v_hf = run("tt", [v_lf, v_j], T.hf[:], T.jc[:], T.lf[:], OP.subtract)
+    v_z = [run("copy", [v_cz, v_lf], T.cz[:, 2:3], T.lf[:]),
+           run("copy", [v_cz, v_lf], T.cz[64:128, 3:4], T.lf[64:128, :])]
+    k_e1 = pack("e1", d)
+    v_h1 = ts([v_hf], T.h1[:], T.hf[:], 64.0, OP.add)
+    sh = {"A": [quant([ll], win("A", 0, 0, P), T.tl[:])], "H": [quant([lc], win("H", 0, 0, P), T.tc[:])]}
+    d = diag(-0.5, [k_e1])
+    v_z += [run("copy", [v_cz, v_hf], T.cz[:, 0:1], T.hf[:]),
+            run("copy", [v_cz, v_h1], T.cz[64:128, 1:2], T.h1[64:128, :])]
+    k_em = pack("em", d)
     sh["B"] = [quant([lr], win("B", 0, 0, P), T.tr[:])]
+    v_e = [run("act", [c_z] + v_z, T.cet[:, t:512:4], T.z128[:], AF.Identity, bias=T.cz[:, t:t + 1]) for t in range(4)]
+    k_u = quant(u4, U, T.ub[:])
 
     free = {(k, b): [] for b in range(4) for k in "ZH"}
 
     def decode_h(t):
         return [mm(sh["H"] + free["H", b] + [k_e1], psH[b][:, 0:P], E["e1"][b], win("H", t, 0, P)) for b in range(4)]
 
-    def decode_z(t):
-        z = []
+    def decode_a(t):
         for b in range(4):
             mm(sh["A"] + free["Z", b] + [k_eq], psZ[b][:, 0:P], E["eq"][b], win("A", t, 0, P), True, False)
+
+    def decode_bh(t):
+        z = []
         for b in range(4):
             mm(sh["B"], psZ[b][:, 0:P], E["eq"][b], win("B", t, 0, P), False, False)
             z.append(mm([k_em], psZ[b][:, 0:P], E["em"][b], win("H", t, 0, P), False, True))
         return z
 
+    decode_a(0)
     tH = decode_h(0)
-    tZ = decode_z(0)
-
-    k_u = quant(u4, U, T.ub[:])
-    v_l = ts([i_p], T.lint[:], T.pint[:], 15, OP.bitwise_and)
-    v_j = run("copy", [i_p], T.jc[:, 0:1], T.pint[:])
-    v_am = ts([i_am], T.am15[:], T.am[:], 15, OP.bitwise_and)
-    v_lf = run("copy", [v_l], T.lf[:], T.lint[:])
-    v_j1 = ts([v_j], T.jc[:, 1:2], T.jc[:, 0:1], 64.0, OP.add)
-    v_cs0 = run("fill", [], T.cst[:], 0.0)
-    v_hf = run("tt", [v_lf, v_j], T.hf[:], T.jc[:, 0:1], T.lf[:], OP.subtract)
-    v_cz = run("fill", [], T.cz[:], 0.0)
-    v_c = [ts([v_am, v_cs0], T.cst[:, t:512:4], T.am15[:], 0.0, OP.is_equal) for t in range(2)]
-    v_h1 = ts([v_hf], T.h1[:], T.hf[:], 64.0, OP.add)
-    v_z = [run("copy", [v_cz, v_hf], T.cz[:, 0:1], T.hf[:]),
-           run("copy", [v_cz, v_lf], T.cz[:, 2:3], T.lf[:]),
-           run("copy", [v_cz, v_lf], T.cz[64:128, 3:4], T.lf[64:128, :]),
-           run("copy", [v_cz, v_h1], T.cz[64:128, 1:2], T.h1[64:128, :])]
-    k_cs = quant(v_c, CS, T.cst[:])
-    v_e = [run("act", [c_z] + v_z, T.cet[:, t:512:4], T.z128[:], AF.Identity, bias=T.cz[:, t:t + 1]) for t in range(4)]
-    v_b0 = ts([i_r, v_hf], T.bm[:, 0:8], T.row16[:, 0:8], T.hf[:], OP.is_equal)
-    v_b1 = ts([i_r, v_h1], T.bm[:, 8:12], T.row16[:, 8:12], T.h1[:], OP.is_equal)
-    v_k = [run("copy", [i_k], T.k192[:, t:192:2], T.k96[:]) for t in range(2)]
-    v_f = [run("fill", [], T.g0[:, P:P + 16], float(P)), run("fill", [], T.g1[:, P:P + 16], float(P)),
-           run("fill", [], T.ot[:, 384:512], 0.0), run("fill", [], T.xt[:], 0.0)]
-    k_ce, k_w = [], []
+    tZ = decode_bh(0)
 
     def send(deps, src, to_right, to_left, t):
         wait("g", deps)
@@ -204,47 +201,63 @@ def rank_program(g, core, T, topo):
             return run("red", [m], T.nsc[:, h:h + 1], bank[:, 0:2], AxisListType.X, OP.max, negate=True,
                        apply_absolute_value=True)
 
+        if t == 0:
+            v_f = [run("fill", [], T.g0[:, P:P + 16], float(P)), run("fill", [], T.g1[:, P:P + 16], float(P)),
+                   run("fill", [], T.ot[:, 384:512], 0.0)]
+            v_k = [run("copy", [i_k], T.k192[:, h:192:2], T.k96[:]) for h in range(2)]
+            k_ce = [quant(v_e, CE, T.cet[:])]
         n0, n1 = T.nsc[:, 0:1], T.nsc[:, 1:2]
-        aA = run("act", [mr], T.sab[:], psH[0][:, 0:P], AF.Abs)
+        aA = [run("act", [mr], T.sab[:, c:e], psH[0][:, c:e], AF.Abs) for c, e in ((0, 128), (128, P))]
         aS = [run("act", [mS[b]], T.stile[:, row[b]], psZ[b][:, 0:P], AF.Copy) for b in range(4)]
+        if last:
+            axo = run("act", list(tx.values()), T.xout[:], XS[R][:], AF.Copy)
+            store("s", [axo], T.xe[:], T.xout[:])
         vc0 = minus(mc0, psH[1], 0)
         vc1 = minus(mc1, psH[2], 1)
-        vd0 = ts([aA, vc0], T.df[:, 0:128], T.sab[:, 0:128], n0, OP.add)
-        vd1 = ts([aA, vc1], T.df[:, 128:P], T.sab[:, 128:P], n1, OP.add)
-        vi0 = ts([aA, vc0], T.g0[:, 128:P], T.sab[:, 128:P], n0, OP.add, 0.0, OP.is_gt)
+        vd0 = ts([aA[0], vc0], T.df[:, 0:128], T.sab[:, 0:128], n0, OP.add)
+        vi1 = ts([aA[0], vc1], T.g1[:, 0:128], T.sab[:, 0:128], n1, OP.add, 0.0, OP.is_ge)
+        vd1 = ts([aA[1], vc1], T.df[:, 128:P], T.sab[:, 128:P], n1, OP.add)
+        vi0 = ts([aA[1], vc0], T.g0[:, 128:P], T.sab[:, 128:P], n0, OP.add, 0.0, OP.is_gt)
         vg0 = run("tt", [vd0, i_t0], T.g0[:, 0:128], T.df[:, 0:128], T.thr[:, 0:128], OP.is_gt)
         vg1 = run("tt", [vd1, i_t1], T.g1[:, 128:P], T.df[:, 128:P], T.thr[:, 128:P], OP.is_gt)
-        vi1 = ts([aA, vc1], T.g1[:, 0:128], T.sab[:, 0:128], n1, OP.add, 0.0, OP.is_ge)
         if t == 0:
-            k_ce.append(quant(v_e, CE, T.cet[:]))
+            v_b = [ts([i_r, v_hf], T.bm[:, 0:8], T.row16[:, 0:8], T.hf[:], OP.is_equal),
+                   ts([i_r, v_h1], T.bm[:, 8:12], T.row16[:, 8:12], T.h1[:], OP.is_equal)]
         vr0 = run("red", [vg0, vi0] + v_f, T.rr[:, 0:1], T.g0[:, 0:P + 1], AxisListType.X, OP.add)
         vr1 = run("red", [vg1, vi1] + v_f, T.rr[:, 1:2], T.g1[:, 0:P + 1], AxisListType.X, OP.add)
-        vo0 = ts([vr0] + v_k, T.ot[:, 0:384:2], T.k192[:], T.rr[:, 0:1], OP.is_equal)
-        vo1 = ts([vr1] + v_k, T.ot[:, 1:384:2], T.k192[:], T.rr[:, 1:2], OP.is_equal)
-        v2 = ts([vr0, vr1], T.t2[:], T.rr[:], -512.0, OP.mult, 122608.0, OP.add)
+        if t == 0:
+            v_b = [ts(v_b, T.below[:], T.bm[:], float(P + K), OP.mult),
+                   ts(v_b, T.above[:], T.bm[:], P + K - 1000000.0, OP.mult, 1000000.0, OP.add),
+                   run("fill", [], T.xt[:], 0.0)]
+        r0, r1 = T.rr[:, 0:1], T.rr[:, 1:2]
+        vo0 = ts([vr0] + v_k, T.ot[:, 0:384:2], T.k192[:], r0, OP.is_equal)
+        vx = [ts([vr0] + v_b, T.xf[:, 0:8], T.below[:, 0:8], r0, OP.is_gt, r0, OP.mult)]
+        vo1 = ts([vr1] + v_k, T.ot[:, 1:384:2], T.k192[:], r1, OP.is_equal)
+        vx.append(ts([vr1] + v_b, T.xf[:, 8:12], T.below[:, 8:12], r1, OP.is_gt, r1, OP.mult))
+        vj = [ts([vr0] + v_b, T.xt[:, e:32:4], T.above[:, 0:8], r0, OP.is_le, c[:], OP.mult) for e, c in ((1, T.hf), (3, T.lf))]
         vqo = quant([vo0, vo1], OQ, T.ot[:])
         me = mm([vqo] + k_ce, psH[3][:, 0:128], CE, OQ)
         S, eo = cols("sq%d" % t, 0, P), T["eo%d" % t]
-        vv = [ts([v2, v_j1], T.vv[:, h:h + 1], T.rr[:, h:h + 1], T.t2[:, h:h + 1], OP.min, T.jc[:, h:h + 1], OP.max)
-              for h in range(2)]
-        vqs = quant(aS, S, T.stile[:])
-        vx = [ts([vv[h], v_b0, v_b1], T.xf[:, c:d], T.bm[:, c:d], T.vv[:, h:h + 1], OP.mult)
-              for h, c, d in ((0, 0, 8), (1, 8, 12))]
-        ve = run("tr", [me], T.etr[:], psH[3][:, 0:96])
         big = 1.5 * 2.0 ** 27
         vh = ts(vx, T.xt[:, 0:48:4], T.xf[:], big, OP.add, big, OP.subtract)
-        veo = run("copy", [ve], eo[:, 0:3], T.etr[:, 0:96:32])
-        vl = run("tt", [vh], T.xt[:, 1:48:4], T.xf[:], T.xt[:, 0:48:4], OP.subtract)
+        vj += [ts([vr1], T.xt[:, 32 + e:48:4], T.above[:, 8:12], r1, OP.is_le, c[:], OP.mult) for e, c in ((1, T.h1), (3, T.lf))]
+        vl = run("tt", [vh], T.xt[:, 2:48:4], T.xf[:], T.xt[:, 0:48:4], OP.subtract)
+        vqs = quant(aS, S, T.stile[:])
         H, X, msg = win("H", t, P, P + K), win("H", t, P + K, P + K + 128), win("H", t, P, SND)
+        ve = run("tr", [me], T.etr[:], psH[3][:, 0:96])
+        vqx = quant([vl, vh] + vj, X, T.xt[:])
+        veo = run("copy", [ve], eo[:, 0:3], T.etr[:, 0:96:32])
         vp = run("copy", [veo, vqs], H[0].bitcast(dt.uint32), S[0].bitcast(dt.uint32).indirect(eo[:, 0:3]))
         ap = run("act", [veo, vqs], H[1], S[1].indirect(eo[:, 0:3]), AF.Copy)
-        vqx = quant([vl, vh], X, T.xt[:])
         da, db = win("A", t, P, SND), win("B", t, P, SND)
         send([vp, vqx], msg[0].bitcast(dt.uint8), da[0].bitcast(dt.uint8), db[0].bitcast(dt.uint8), t)
         send([ap, vqx], msg[1], da[1], db[1], t)
         ach = [run("act", [ve], T.chs[0:1, K * t + 16 * m:K * t + 16 * m + 16], psH[3][0:1, 32 * m:32 * m + 16], AF.Copy)
                for m in range(3)]
         chtok.append(ach[-1])
+        if t == 0:
+            v_c = [ts([v_am], T.cst[:, h:512:4], T.am15[:], 0.0, OP.is_equal) for h in range(4)]
+            k_cs = quant(v_c, CS, T.cst[:])
 
         def places(k, deps, bank, tile, c):
             m = mm(deps + [k_cs], bank[:, 0:128], CS, tile)
@@ -257,14 +270,12 @@ def rank_program(g, core, T, topo):
 
         vsh = places("H", [vqx, aS[0]], psZ[0], X, 0)()
         sh["H"] = pick("H", [vsh, vp, ap])
-        for b, d in enumerate(([aA], [vc0], [vc1], ach + [ve])):
+        for b, d in enumerate((aA, [vc0], [vc1], ach + [ve])):
             free["H", b] = d
         if not last:
             tH = decode_h(t + 1)
         else:
-            k_w.append(quant([lw], cols("wq", 0, 128), T.tw[:]))
-            axo = run("act", list(tx.values()), T.xout[:], XS[R][:], AF.Copy)
-            store("s", [axo], T.xe[:], T.xout[:])
+            k_w = quant([lw], cols("wq", 0, 128), T.tw[:])
             store("s", chtok, T.ch[:], T.chs[0:1, :])
             store("s", sh["H"], T.oc[:, 4 * P:8 * P], T.fin[:, P:2 * P].bitcast(dt.uint8))
         ra, rb = ("rA%d" % t, got["A"]), ("rB%d" % t, got["B"])
@@ -277,9 +288,10 @@ def rank_program(g, core, T, topo):
         for b, d in enumerate((vsh, aS[1], vsa, vsb)):
             free["Z", b] = [d]
         if not last:
-            tZ = decode_z(t + 1)
+            decode_a(t + 1)
+            tZ = decode_bh(t + 1)
 
-    my = mm(sh["A"] + free["Z", 0] + k_w, psZ[0][:, 0:P], cols("wq", 0, 128), win("A", R, 0, P))
+    my = mm(sh["A"] + free["Z", 0] + [k_w], psZ[0][:, 0:P], cols("wq", 0, 128), win("A", R, 0, P))
     vy = run("copy", [my], T.yout[:], psZ[0][:, 0:P])
     store("s", sh["A"], T.oc[:, 0:4 * P], T.fin[:, 0:P].bitcast(dt.uint8))
     store("s", sh["B"], T.oc[:, 8 * P:12 * P], T.fin[:, 2 * P:3 * P].bitcast(dt.uint8))

from concourse.bass import DstId, RemoteDMATransfer
from concourse.mybir import dt, AluOpType as OP, AxisListType, ActivationFunctionType as AF

P, K, R = 192, 48, 3
BF, F32, I32, U16, FP8, U8 = "bfloat16", "float32", "int32", "uint16", "float8_e4m3fn_x4", "uint8"
SND = P + K + 12
STEPS = "x0 x1 d0 x2 d1 x3 d2 d3"

SCRATCH = {}
SCRATCH.update({n: ("sbuf", [128, w], BF) for n, w in dict(
    x0=768, x1=768, x2=768, x3=768, tl=768, tc=768, tr=768, tu=4, tw=512, ub=512, ones=128, ident=128, z128=128, stage=2048,
    cet=512, cst=512, thr=192, k96=96, k192=192, dtile=768, stile=768, g0=208, g1=208, ot=512, xt=512).items()})
SCRATCH.update({n: ("sbuf", [128, w], F32) for n, w in dict(
    lf=1, hf=1, h1=1, jc=1, cz=4, row16=12, bm=12, below=12, above=12, sab=192, nsc=2, df=192, rr=2, xf=12, etr=96,
    chs=R * K, xout=768, yout=192).items()})
SCRATCH.update({n: ("sbuf", [128, w], I32) for n, w in dict(pint=1, lint=1, am=128, am15=128).items()})
_Q = dict(uq=128, wq=128, e1=512, eq=512, em=512, ce=128, cs=128, dq=P, oq=128, fin=3 * P)
for _t in range(R):
    _Q.update({"wA%d" % _t: SND, "wB%d" % _t: SND, "wH%d" % _t: P + K + 128, "sq%d" % _t: P})
    SCRATCH["eo%d" % _t] = ("sbuf", [128, 4], U16)
    for _n in "AHB":
        SCRATCH["so%s%d" % (_n, _t)] = ("sbuf", [128, 12], U16)
for _n, _w in _Q.items():
    SCRATCH[_n] = ("sbuf", [128, _w], FP8)
    SCRATCH[_n + "_s"] = ("sbuf", [128, _w], U8)
for _b in range(4):
    SCRATCH["psZ%d" % _b] = ("psum", [128, 512], F32)
    SCRATCH["psH%d" % _b] = ("psum", [128, 512], F32)

SEMAPHORES = (["sv", "sa", "st", "sg", "left", "lc", "ll", "lr", "lx", "lu", "lw", "out"]
              + ["rA%d" % t for t in range(R)] + ["rB%d" % t for t in range(R)])


def rank_program(g, core, T, topo):
    rank = T.rank_of(core)
    if rank is None:
        return
    n = len(T.cores)
    right, left = T.cores[(rank + 1) % n], T.cores[(rank - 1) % n]
    Q = {"v": g.vector, "a": g.scalar, "t": g.tensor, "g": g, "s": g.sync}
    cnt = {"v": 0, "a": 0, "t": 0, "g": 0}
    seen = {q: {} for q in Q}
    total = {"out": 0, "left": 0}

    def wait(q, deps):
        need = {}
        for s, v in deps:
            need[s] = max(v, need.get(s, 0))
        for s, v in need.items():
            if seen[q].get(s, 0) < v:
                Q[q].wait_ge(T.sem[s], v)
                seen[q][s] = v

    CALLS = {"act": g.scalar.activation, "mm": g.tensor.matmul_mx, "quant": g.vector.quantize_mx, "copy": g.vector.tensor_copy,
             "tt": g.vector.tensor_tensor, "ts": g.vector.tensor_scalar, "red": g.vector.tensor_reduce,
             "tr": g.vector.transpose, "fill": g.vector.memset, "iota": g.iota, "select": g.affine_select}
    QUEUE = {"act": "a", "mm": "t", "iota": "g", "select": "g"}

    def run(name, deps, *args, **kw):
        q = QUEUE.get(name, "v")
        wait(q, deps)
        CALLS[name](*args, **kw).then_inc(T.sem["s" + q], 1)
        cnt[q] += 1
        return ("s" + q, cnt[q])

    def load(q, sem, out, in_):
        Q[q].dma_start(out, in_).then_inc(T.sem[sem], 16)
        return (sem, 16)

    def store(q, deps, out, in_):
        wait(q, deps)
        Q[q].dma_start(out, in_).then_inc(T.sem.out, 16)
        total["out"] += 16

    def ts(deps, out, in0, s1, op0, s2=None, op1=None):
        kw = {} if op1 is None else {"op1": op1}
        return run("ts", deps, out=out, in0=in0, scalar1=s1, scalar2=s2, op0=op0, **kw)

    def cols(name, a, b):
        return T[name][:, a:b], T[name + "_s"][:, a:b]

    def win(k, t, a, b):
        o = P * "AHB".index(k)
        return cols("fin", o + a, o + b) if t == R else cols("w%s%d" % (k, t), a, b)

    def mm(deps, out, l, r, start=True, stop=True):
        return run("mm", deps, out, l[0], l[1], r[0], r[1], start, stop)

    def quant(deps, q, tile):
        return run("quant", deps, q[0], q[1], tile)

    psZ = [T["psZ%d" % b] for b in range(4)]
    psH = [T["psH%d" % b] for b in range(4)]
    XS = [T.x0, T.x1, T.x2, T.x3]
    U, DQ, CE, CS, OQ = cols("uq", 0, 128), cols("dq", 0, P), cols("ce", 0, 128), cols("cs", 0, 128), cols("oq", 0, 128)
    E = {c: [cols(c, 128 * b, 128 * b + 128) for b in range(4)] for c in ("e1", "eq", "em")}
    row = [slice(b, 4 * P, 4) for b in range(4)]

    ll = load("a", "ll", T.tl[:], T.hl[:])
    lc = load("s", "lc", T.tc[:], T.hc[:])
    lu = load("s", "lu", T.tu[:], T.u[:, 0:4])
    lr = load("s", "lr", T.tr[:], T.hr[:])
    lx = load("a", "lx", T.x0[:], T.x[:])
    lw = load("s", "lw", T.tw[:], T.w[:])

    small = {"allow_small_or_imprecise_dtypes": True}
    c_ones = run("fill", [], T.ones[:], 1.0)
    i_p = run("iota", [], T.pint[:], [[0, 1]], 0, 1)
    c_id = run("select", [c_ones], T.ident[:], T.ones[:], [[-1, 128]], OP.is_equal, 0.0, 0, 1)
    c_stage = run("fill", [], T.stage[:], 0.0)
    c_z = run("fill", [], T.z128[:], 0.0)
    i_am = run("iota", [], T.am[:], [[1, 128]], 128, -1)
    i_k = run("iota", [], T.k96[:], [[16, 3], [0, 2], [1, 16]], P, 0, **small)
    i_r = run("iota", [], T.row16[:], [[16, 12]], 0, 0, **small)
    tiny = -(2.0 ** -120)
    i_t0 = run("select", [c_z], T.thr[:, 0:128], T.z128[:], [[1, 128]], OP.is_ge, tiny, 0, -1)
    i_t1 = run("select", [c_z], T.thr[:, 128:P], T.z128[:, 0:64], [[1, 64]], OP.is_ge, tiny, 64, -1)

    def diag(c, before):
        return [ts([c_id, c_stage] + before, T.stage[:, 512 * b + b:512 * (b + 1):4], T.ident[:], c, OP.mult) for b in range(4)]

    def pack(name, d):
        return quant(d, cols(name, 0, 512), T.stage[:])

    u4 = [run("act", [lu, c_z], T.ub[:, t:512:4], T.z128[:], AF.Identity, bias=T.tu[:, t:t + 1]) for t in range(4)]
    d = diag(0.25, [])
    v_l = ts([i_p], T.lint[:], T.pint[:], 15, OP.bitwise_and)
    v_j = run("copy", [i_p], T.jc[:], T.pint[:])
    v_cz = run("fill", [], T.cz[:], 0.0)
    k_eq = pack("eq", d)
    v_lf = run("copy", [v_l], T.lf[:], T.lint[:])
    v_am = ts([i_am], T.am15[:], T.am[:], 15, OP.bitwise_and)
    d = diag(1.0, [k_eq])
    v_hf = run("tt", [v_lf, v_j], T.hf[:], T.jc[:], T.lf[:], OP.subtract)
    v_z = [run("copy", [v_cz, v_lf], T.cz[:, 2:3], T.lf[:]),
           run("copy", [v_cz, v_lf], T.cz[64:128, 3:4], T.lf[64:128, :])]
    k_e1 = pack("e1", d)
    v_h1 = ts([v_hf], T.h1[:], T.hf[:], 64.0, OP.add)
    sh = {"A": [quant([ll], win("A", 0, 0, P), T.tl[:])], "H": [quant([lc], win("H", 0, 0, P), T.tc[:])]}
    d = diag(-0.5, [k_e1])
    v_z += [run("copy", [v_cz, v_hf], T.cz[:, 0:1], T.hf[:]),
            run("copy", [v_cz, v_h1], T.cz[64:128, 1:2], T.h1[64:128, :])]
    k_em = pack("em", d)
    sh["B"] = [quant([lr], win("B", 0, 0, P), T.tr[:])]
    v_e = [run("act", [c_z] + v_z, T.cet[:, t:512:4], T.z128[:], AF.Identity, bias=T.cz[:, t:t + 1]) for t in range(4)]
    k_u = quant(u4, U, T.ub[:])

    free = {(k, b): [] for b in range(4) for k in "ZH"}

    def decode_h(t):
        return [mm(sh["H"] + free["H", b] + [k_e1], psH[b][:, 0:P], E["e1"][b], win("H", t, 0, P)) for b in range(4)]

    def decode_a(t):
        for b in range(4):
            mm(sh["A"] + free["Z", b] + [k_eq], psZ[b][:, 0:P], E["eq"][b], win("A", t, 0, P), True, False)

    def decode_bh(t):
        z = []
        for b in range(4):
            mm(sh["B"], psZ[b][:, 0:P], E["eq"][b], win("B", t, 0, P), False, False)
            z.append(mm([k_em], psZ[b][:, 0:P], E["em"][b], win("H", t, 0, P), False, True))
        return z

    decode_a(0)
    tH = decode_h(0)
    tZ = decode_bh(0)

    def send(deps, src, to_right, to_left, t):
        wait("g", deps)
        tr = []
        for who, dst, sem, odd in ((right, to_right, "rA%d" % t, 0), (left, to_left, "rB%d" % t, 1)):
            rid, pid, _ = topo.addr(who)
            eng = topo.engines(core, who)[odd::2]
            tr.append(RemoteDMATransfer(dst_ids=[DstId(rid=rid, pnc=pid)], dma_engine_mask=sum(1 << e for e in eng),
                                        remote_sem=T.sem[sem], src=src, dst=dst))
            total["left"] += len(eng)
        g.remote_dma_fused(tr, local_sem=T.sem.left)

    got = {"A": 2 * len(topo.engines(left, core)[0::2]), "B": 2 * len(topo.engines(right, core)[1::2])}
    chtok = []

    for t in range(R):
        last = t == R - 1
        tx, td = {}, {}
        for step in STEPS.split():
            b = int(step[1])
            x = XS[t + 1][:, row[b]]
            if step[0] == "x":
                tx[b] = run("tt", [tZ[b], lx], x, psZ[b][:, 0:P], XS[t][:, row[b]], OP.add)
            else:
                td[b] = run("tt", [tx[b], tH[b]], T.dtile[:, row[b]], x, psH[b][:, 0:P], OP.subtract)
        tq = quant(list(td.values()), DQ, T.dtile[:])
        for b in range(4):
            mm([tx[b]], psZ[b][:, 0:P], E["e1"][b], win("H", t, 0, P), True, False)
        mr = mm([tq, k_u], psH[0][:, 0:P], U, DQ)
        mc0 = mm([tq], psH[1][:, 0:128], cols("dq", 0, 128), U)
        mc1 = mm([tq], psH[2][:, 0:128], cols("dq", 64, 192), U)
        mS = [mm([tq], psZ[b][:, 0:P], E["e1"][b], DQ, False, True) for b in range(4)]

        def minus(m, bank, h):
            return run("red", [m], T.nsc[:, h:h + 1], bank[:, 0:2], AxisListType.X, OP.max, negate=True,
                       apply_absolute_value=True)

        if t == 0:
            v_f = [run("fill", [], T.g0[:, P:P + 16], float(P)), run("fill", [], T.g1[:, P:P + 16], float(P)),
                   run("fill", [], T.ot[:, 384:512], 0.0)]
            v_k = [run("copy", [i_k], T.k192[:, h:192:2], T.k96[:]) for h in range(2)]
            k_ce = [quant(v_e, CE, T.cet[:])]
        n0, n1 = T.nsc[:, 0:1], T.nsc[:, 1:2]
        aA = [run("act", [mr], T.sab[:, c:e], psH[0][:, c:e], AF.Abs) for c, e in ((0, 128), (128, P))]
        aS = [run("act", [mS[b]], T.stile[:, row[b]], psZ[b][:, 0:P], AF.Copy) for b in range(4)]
        if last:
            axo = run("act", list(tx.values()), T.xout[:], XS[R][:], AF.Copy)
            store("s", [axo], T.xe[:], T.xout[:])
        vc0 = minus(mc0, psH[1], 0)
        vc1 = minus(mc1, psH[2], 1)
        vd0 = ts([aA[0], vc0], T.df[:, 0:128], T.sab[:, 0:128], n0, OP.add)
        vi1 = ts([aA[0], vc1], T.g1[:, 0:128], T.sab[:, 0:128], n1, OP.add, 0.0, OP.is_ge)
        vd1 = ts([aA[1], vc1], T.df[:, 128:P], T.sab[:, 128:P], n1, OP.add)
        vi0 = ts([aA[1], vc0], T.g0[:, 128:P], T.sab[:, 128:P], n0, OP.add, 0.0, OP.is_gt)
        vg0 = run("tt", [vd0, i_t0], T.g0[:, 0:128], T.df[:, 0:128], T.thr[:, 0:128], OP.is_gt)
        vg1 = run("tt", [vd1, i_t1], T.g1[:, 128:P], T.df[:, 128:P], T.thr[:, 128:P], OP.is_gt)
        if t == 0:
            v_b = [ts([i_r, v_hf], T.bm[:, 0:8], T.row16[:, 0:8], T.hf[:], OP.is_equal),
                   ts([i_r, v_h1], T.bm[:, 8:12], T.row16[:, 8:12], T.h1[:], OP.is_equal)]
        vr0 = run("red", [vg0, vi0] + v_f, T.rr[:, 0:1], T.g0[:, 0:P + 1], AxisListType.X, OP.add)
        vr1 = run("red", [vg1, vi1] + v_f, T.rr[:, 1:2], T.g1[:, 0:P + 1], AxisListType.X, OP.add)
        if t == 0:
            v_b = [ts(v_b, T.below[:], T.bm[:], float(P + K), OP.mult),
                   ts(v_b, T.above[:], T.bm[:], P + K - 1000000.0, OP.mult, 1000000.0, OP.add),
                   run("fill", [], T.xt[:], 0.0)]
        r0, r1 = T.rr[:, 0:1], T.rr[:, 1:2]
        vo0 = ts([vr0] + v_k, T.ot[:, 0:384:2], T.k192[:], r0, OP.is_equal)
        vx = [ts([vr0] + v_b, T.xf[:, 0:8], T.below[:, 0:8], r0, OP.is_gt, r0, OP.mult)]
        vo1 = ts([vr1] + v_k, T.ot[:, 1:384:2], T.k192[:], r1, OP.is_equal)
        vx.append(ts([vr1] + v_b, T.xf[:, 8:12], T.below[:, 8:12], r1, OP.is_gt, r1, OP.mult))
        vj = [ts([vr0] + v_b, T.xt[:, e:32:4], T.above[:, 0:8], r0, OP.is_le, c[:], OP.mult) for e, c in ((1, T.hf), (3, T.lf))]
        vqo = quant([vo0, vo1], OQ, T.ot[:])
        me = mm([vqo] + k_ce, psH[3][:, 0:128], CE, OQ)
        S, eo = cols("sq%d" % t, 0, P), T["eo%d" % t]
        big = 1.5 * 2.0 ** 27
        vh = ts(vx, T.xt[:, 0:48:4], T.xf[:], big, OP.add, big, OP.subtract)
        vj += [ts([vr1], T.xt[:, 32 + e:48:4], T.above[:, 8:12], r1, OP.is_le, c[:], OP.mult) for e, c in ((1, T.h1), (3, T.lf))]
        vl = run("tt", [vh], T.xt[:, 2:48:4], T.xf[:], T.xt[:, 0:48:4], OP.subtract)
        vqs = quant(aS, S, T.stile[:])
        H, X, msg = win("H", t, P, P + K), win("H", t, P + K, P + K + 128), win("H", t, P, SND)
        ve = run("tr", [me], T.etr[:], psH[3][:, 0:96])
        vqx = quant([vl, vh] + vj, X, T.xt[:])
        veo = run("copy", [ve], eo[:, 0:3], T.etr[:, 0:96:32])
        vp = run("copy", [veo, vqs], H[0].bitcast(dt.uint32), S[0].bitcast(dt.uint32).indirect(eo[:, 0:3]))
        ap = run("act", [veo, vqs], H[1], S[1].indirect(eo[:, 0:3]), AF.Copy)
        da, db = win("A", t, P, SND), win("B", t, P, SND)
        send([vp, vqx], msg[0].bitcast(dt.uint8), da[0].bitcast(dt.uint8), db[0].bitcast(dt.uint8), t)
        send([ap, vqx], msg[1], da[1], db[1], t)
        ach = [run("act", [ve], T.chs[0:1, K * t + 16 * m:K * t + 16 * m + 16], psH[3][0:1, 32 * m:32 * m + 16], AF.Copy)
               for m in range(3)]
        chtok.append(ach[-1])
        if t == 0:
            v_c = [ts([v_am], T.cst[:, h:512:4], T.am15[:], 0.0, OP.is_equal) for h in range(4)]
            k_cs = quant(v_c, CS, T.cst[:])

        def places(k, deps, bank, tile, c):
            m = mm(deps + [k_cs], bank[:, 0:128], CS, tile)
            return lambda: run("copy", [m], T["so%s%d" % (k, t)][:], bank[:, c:c + 12])

        def pick(k, deps):
            so, d, w = T["so%s%d" % (k, t)], win(k, t + 1, 0, P), cols("w%s%d" % (k, t), 0, SND)
            return [run("copy", deps, d[0].bitcast(dt.uint32), w[0].bitcast(dt.uint32).indirect(so[:])),
                    run("act", deps, d[1], w[1].indirect(so[:]), AF.Copy)]

        vsh = places("H", [vqx, aS[0]], psZ[0], X, 0)()
        sh["H"] = pick("H", [vsh, vp, ap])
        for b, d in enumerate((aA, [vc0], [vc1], ach + [ve])):
            free["H", b] = d
        if not last:
            tH = decode_h(t + 1)
        else:
            k_w = quant([lw], cols("wq", 0, 128), T.tw[:])
            store("s", chtok, T.ch[:], T.chs[0:1, :])
            store("s", sh["H"], T.oc[:, 4 * P:8 * P], T.fin[:, P:2 * P].bitcast(dt.uint8))
        ra, rb = ("rA%d" % t, got["A"]), ("rB%d" % t, got["B"])
        la = places("A", [ra, aS[2]], psZ[2], win("A", t, SND - 128, SND), 116)
        lb = places("B", [rb, aS[3]], psZ[3], win("B", t, SND - 128, SND), 116)
        vsa = la()
        sh["A"] = pick("A", [vsa, ra])
        vsb = lb()
        sh["B"] = pick("B", [vsb, rb])
        for b, d in enumerate((vsh, aS[1], vsa, vsb)):
            free["Z", b] = [d]
        if not last:
            decode_a(t + 1)
            tZ = decode_bh(t + 1)

    my = mm(sh["A"] + free["Z", 0] + [k_w], psZ[0][:, 0:P], cols("wq", 0, 128), win("A", R, 0, P))
    vy = run("copy", [my], T.yout[:], psZ[0][:, 0:P])
    store("s", sh["A"], T.oc[:, 0:4 * P], T.fin[:, 0:P].bitcast(dt.uint8))
    store("s", sh["B"], T.oc[:, 8 * P:12 * P], T.fin[:, 2 * P:3 * P].bitcast(dt.uint8))
    for k in range(4):
        store("a" if k % 2 else "s", sh["A"] + sh["B"] + sh["H"], T.osc[4 * k:4 * k + 4, :], T.fin_s[32 * k:32 * k + 4, :])
    store("a", [vy], T.y[:], T.yout[:])
    wait("g", [("s" + q, c) for q, c in cnt.items()] + list(total.items()))
